import numpy as np
import ml_dtypes


def mxq(x, axis, fmt="e4m3"):
    dtype, down = {"e4m3": (ml_dtypes.float8_e4m3fn, 7), "e5m2": (ml_dtypes.float8_e5m2, 14)}[fmt]
    v = np.moveaxis(np.asarray(x, np.float32).astype(ml_dtypes.bfloat16).astype(np.float64), axis, -1)
    blocks = v.reshape(v.shape[:-1] + (-1, 32))
    amax = np.abs(blocks).max(-1, keepdims=True)
    byte = np.maximum(np.where(amax > 0, np.frexp(amax)[1] - 1 + 127, 0) - down, 1)
    scale = np.exp2(byte - 127.0)
    codes = (blocks / scale).astype(np.float32).astype(dtype).astype(np.float64)
    return np.moveaxis((codes * scale).reshape(v.shape), -1, axis)


WIDE = False


def mx_kscale(k):
    if not WIDE:
        return np.ones(k)
    levels = np.array([10, -10, 5, -5, 0])
    if k % 512:
        return np.exp2(np.random.permutation(np.resize(levels, k // 32))).repeat(32)
    a = np.empty((k // 512, 16))
    for p in range(k // 512):
        a[p, :8] = np.random.permutation(np.resize(levels, 8))
        for g in range(8):
            far = levels[np.abs(levels - a[p, g]) >= 10]
            a[p, g + 8] = far[np.random.randint(len(far))]
    return np.exp2(a.ravel()).repeat(32)


def f64(x):
    return np.asarray(x).astype(np.float64)


def striped(idx):
    return np.tile(np.asarray(idx).reshape(-1, 16).T, (8, 1)).astype(np.uint16)


def unstriped(offs):
    return offs[:16].T.reshape(-1).astype(np.int64)


E2M1 = np.array([0.0, 0.5, 1.0, 1.5, 2.0, 3.0, 4.0, 6.0, -0.0, -0.5, -1.0, -1.5, -2.0, -3.0, -4.0, -6.0])


def pack_weight(w, fmt):
    k, n = w.shape
    w = f64(np.asarray(w, np.float32).astype(ml_dtypes.bfloat16)).reshape(k // 32, 32, n)
    amax = np.abs(w).max(1)
    if fmt == "e4m3":
        byte = np.frexp(amax)[1] - 1 + 127 - 7
    else:
        mant, ex = np.frexp(amax / 6.0)
        byte = np.where(mant > 0.5, ex, ex - 1) + 127
    byte = np.clip(np.where(amax > 0, byte, 1), 1, 254)
    scaled = (w * np.exp2(127.0 - byte)[:, None, :]).reshape(k, n).astype(np.float32)
    by_word = np.ascontiguousarray(scaled.reshape(k // 512, 128, 4, n).transpose(0, 1, 3, 2))
    if fmt == "e4m3":
        words = by_word.astype(ml_dtypes.float8_e4m3fn).view(np.uint8)
    else:
        c = by_word.astype(ml_dtypes.float4_e2m1fn).view(np.uint8) & 0xF
        words = (c[..., 0::2] | (c[..., 1::2] << 4)).reshape(k // 512, 128, 2 * n)
    return np.ascontiguousarray(words), np.ascontiguousarray(byte.astype(np.uint8).reshape(k // 512, 16, n))


def unpack_weight(words, scales, fmt):
    g, _, n = scales.shape
    words = np.ascontiguousarray(words).reshape(g, 128, n, -1)
    if fmt == "e4m3":
        vals = words.view(ml_dtypes.float8_e4m3fn).astype(np.float64)
    else:
        nib = np.empty((g, 128, n, 4), np.uint8)
        nib[..., 0::2] = words & 0xF
        nib[..., 1::2] = words >> 4
        vals = E2M1[nib]
    vals = vals * np.repeat(np.exp2(scales.astype(np.float64) - 127.0), 8, axis=1)[..., None]
    return vals.transpose(0, 1, 3, 2).reshape(g * 512, n)


D, T, I, Q, K, M = 512, 2048, 512, 128, 16, 2048


def setup_inputs():
    n = np.random.standard_normal
    idx = np.random.permutation(T)[:I]
    idx2 = np.random.permutation(M)[:I]
    fd = mx_kscale(D)
    keysp = pack_weight(n((D, T)) / fd[:, None], "e2m1")
    return {
        "query": (n((D, Q)) * 1.0 / np.sqrt(D) * fd[:, None]).astype(np.float32),
        "keys_words": keysp[0],
        "keys_scales": keysp[1],
        "lowend": np.tile(np.random.uniform(-1.5, 0.0, T), (128, 1)).astype(np.float32),
        "highend": np.tile(np.random.uniform(0.0, 1.5, T), (128, 1)).astype(np.float32),
        "lam": (np.random.uniform(0.8, 2.0, (Q, 1))).astype(np.float32),
        "old": (np.random.uniform(0.0, 2.0, (Q, M))).astype(np.float32),
        "fade": (np.random.uniform(0.3, 0.9, (Q, 1))).astype(np.float32),
        "offs": striped(idx),
        "offs2": striped(idx2),
    }


def reference(query, keys_words, keys_scales, lowend, highend, lam, old, fade, offs, offs2):
    idx = unstriped(offs)
    idx2 = unstriped(offs2)
    keysu = unpack_weight(keys_words, keys_scales, "e2m1")
    queryq = mxq(f64(query), 0, "e4m3")
    keysidxg = keysu[:, idx]
    a = queryq.T @ keysidxg
    s = np.minimum(a - f64(lowend)[:1][:, idx], f64(highend)[:1][:, idx] - a) * f64(lam)
    p = np.exp(s - np.max(s, axis=1, keepdims=True))
    r = p / np.sum(p, axis=1, keepdims=True)
    rt = r.T
    rg = rt.reshape(I, K, Q // K).sum(axis=2)
    rq = 1.0 / np.sqrt(rg)
    rr = np.repeat(rq, Q // K, axis=1)
    w0 = rt * rr
    w = w0.T
    ws = w * 128.0
    wf = np.zeros((Q, M))
    wf[:, idx2] = ws
    y = f64(old) * f64(fade) + wf
    return y

@@ -1,0 +1,203 @@
+from contextlib import ExitStack
+
+import concourse.mybir as mybir
+from concourse.masks import make_identity
+
+D, T, I, Q, K, M = 512, 2048, 512, 128, 16, 2048
+
+F32 = mybir.dt.float32
+BF16 = mybir.dt.bfloat16
+I32 = mybir.dt.int32
+U32 = mybir.dt.uint32
+U16 = mybir.dt.uint16
+U8 = mybir.dt.uint8
+FP8X4 = mybir.dt.float8_e4m3fn_x4
+FP4X4 = mybir.dt.float4_e2m1fn_x4
+ALU = mybir.AluOpType
+ACT = mybir.ActivationFunctionType
+AX = mybir.AxisListType
+
+P = 128
+PACK = 4
+HALF = I // 2
+GROUP = Q // K
+ROW = P - 1
+OUT_COLS = [256, 512, 512, 512, 256]
+
+FLOPS = 2 * D * Q * I
+BYTES = 4 * D * Q + 2 * P * T + 16 * T + 2 * 4 * T + 2 * 4 * Q + 2 * 4 * Q * M + 2 * 2 * P * (I // 16)
+
+
+def tile_attend_interval_balanced_counts_kernel(tc, query, keys_words, keys_scales, lowend, highend, lam, old, fade, offs, offs2, out):
+    nc = tc.nc
+    with ExitStack() as ctx:
+        sb = ctx.enter_context(tc.tile_pool(name="sb", bufs=1))
+        ps = ctx.enter_context(tc.psum_pool(name="ps", bufs=1))
+
+        def bank(n, name):
+            return ps.tile([P, 512], F32, name=name, tag="bank%d" % n)
+
+        offs_sb = sb.tile([P, I // 16], U16, name="offs_sb")
+        offs2_sb = sb.tile([P, I // 16], U16, name="offs2_sb")
+        scale_win = sb.tile([P, T], U8, name="scale_win")
+        word_win = sb.tile([P, T], U16, name="word_win")
+        low_win = sb.tile([P, T], F32, name="low_win", tag="low_then_old")
+        high_win = sb.tile([P, T], F32, name="high_win", tag="high_then_fade")
+        q_raw = sb.tile([P, PACK, Q], F32, name="q_raw", tag="query_then_lam")
+        ident = sb.tile([P, P], F32, name="ident")
+
+        nc.vector.memset(scale_win[:].bitcast(I32), 0)
+        nc.vector.memset(low_win[0:ROW, :], 0.0)
+        nc.vector.memset(high_win[0:ROW, :], 0.0)
+        make_identity(nc, ident[:])
+
+        nc.sync.dma_start(offs_sb[:], offs)
+        nc.sync.dma_start(out=q_raw[:], in_=query.rearrange("(p j) q -> p j q", j=PACK))
+        nc.sync.dma_start(out=word_win[:].bitcast(I32), in_=keys_words[0].bitcast(I32))
+        nc.scalar.dma_start(out=low_win[ROW:P, :], in_=lowend[0:1, :])
+        nc.scalar.dma_start(out=high_win[ROW:P, :], in_=highend[0:1, :])
+        for quad in range(4):
+            nc.sync.dma_start(
+                out=scale_win[32 * quad : 32 * quad + 4, :].bitcast(I32),
+                in_=keys_scales[0, 4 * quad : 4 * quad + 4, :].bitcast(I32),
+            )
+        nc.sync.dma_start(offs2_sb[:], offs2)
+
+        def half_of(list_tile, h):
+            return list_tile[:, h * (HALF // 16) : (h + 1) * (HALF // 16)]
+
+        q_bf = sb.tile([P, Q, PACK], BF16, name="q_bf", tag="q_bf_then_counts", align_bytes=64)
+        q_codes = sb.tile([P, Q], U32, name="q_codes", align_bytes=64)
+        q_scales = sb.tile([P, Q], U8, name="q_scales", align_bytes=64)
+        nc.scalar.copy(q_bf[:], q_raw[:].rearrange("p j q -> p q j"))
+        lam_sb = sb.tile([P, 1], F32, name="lam_sb", tag="query_then_lam")
+        nc.sync.dma_start(out=lam_sb[:], in_=lam)
+
+        lows = [sb.tile([P, HALF], F32, name="low%d" % h) for h in range(2)]
+        highs = [sb.tile([P, HALF], F32, name="high%d" % h) for h in range(2)]
+        nc.vector.tensor_copy(lows[0][:], low_win[:].indirect(half_of(offs_sb, 0)))
+        nc.scalar.activation(highs[0][:], high_win[:].indirect(half_of(offs_sb, 0)), ACT.Copy)
+        nc.scalar.activation(lows[1][:], low_win[:].indirect(half_of(offs_sb, 1)), ACT.Copy)
+        nc.scalar.activation(highs[1][:], high_win[:].indirect(half_of(offs_sb, 1)), ACT.Copy)
+        old_sb = sb.tile([P, M], F32, name="old_sb", tag="low_then_old")
+        nc.sync.dma_start(out=old_sb[:], in_=old)
+        fade_sb = sb.tile([P, 1], F32, name="fade_sb", tag="high_then_fade")
+        nc.sync.dma_start(out=fade_sb[:], in_=fade)
+
+        nc.vector.quantize_mx(out=q_codes[:].bitcast(FP8X4), scales=q_scales[:], in_=q_bf[:].rearrange("p q j -> p (q j)"))
+        words = []
+        scales = []
+        for h in range(2):
+            key_words = sb.tile([P, HALF], U16, name="key_words%d" % h, align_bytes=64)
+            nc.vector.tensor_copy(key_words[:], word_win[:].indirect(half_of(offs_sb, h)))
+            words.append(key_words)
+            key_scales = sb.tile([P, HALF], U8, name="key_scales%d" % h, align_bytes=64)
+            nc.vector.tensor_copy(key_scales[:], scale_win[:].indirect(half_of(offs_sb, h)))
+            scales.append(key_scales)
+
+        placed = sb.tile([P, M], F32, name="placed", tag="q_bf_then_counts", align_bytes=64)
+        nc.gpsimd.memset(placed[:], 0.0)
+
+        neg_s = sb.tile([P, I], F32, name="neg_s")
+        neg_max = []
+        for h in range(2):
+            ends_t = bank(h, "ends_t%d" % h)
+            for c in range(2):
+                nc.tensor.transpose(ends_t[:, c * P : (c + 1) * P], lows[h][:, c * P : (c + 1) * P], ident[:])
+            for c in range(2):
+                nc.tensor.transpose(ends_t[:, (2 + c) * P : (3 + c) * P], highs[h][:, c * P : (c + 1) * P], ident[:])
+            neg_half_ends = sb.tile([P, 4], F32, name="neg_half_ends%d" % h)
+            nc.scalar.activation(neg_half_ends[:], ends_t[:, ROW::P], ACT.Copy, scale=-0.5)
+            neg_centre = sb.tile([P, 2], F32, name="neg_centre%d" % h)
+            neg_radius = sb.tile([P, 2], F32, name="neg_radius%d" % h)
+            nc.vector.tensor_tensor(neg_centre[:], neg_half_ends[:, 2:4], neg_half_ends[:, 0:2], ALU.add)
+            nc.vector.tensor_tensor(neg_radius[:], neg_half_ends[:, 2:4], neg_half_ends[:, 0:2], ALU.subtract)
+
+            neg_margin = bank(6 + h, "neg_margin%d" % h)
+            for c in range(2):
+                nc.tensor.matmul(
+                    neg_margin[:, c * P : (c + 1) * P],
+                    lhsT=neg_radius[:, c : c + 1].to_broadcast([P, P]),
+                    rhs=ident[:],
+                    is_transpose=True,
+                    start=(c == 0),
+                    stop=False,
+                )
+            for c in range(2):
+                prod = bank(2 + 2 * h + c, "prod%d%d" % (h, c))
+                nc.tensor.matmul_mx(
+                    out=prod[:, 0:Q],
+                    lhsT=words[h][:, c * P : (c + 1) * P].bitcast(FP4X4),
+                    lhsT_scale=scales[h][:, c * P : (c + 1) * P],
+                    rhs=q_codes[:].bitcast(FP8X4),
+                    rhs_scale=q_scales[:],
+                    start=True,
+                    stop=True,
+                )
+                dist = sb.tile([P, Q], F32, name="dist%d%d" % (h, c))
+                nc.scalar.activation(dist[:], prod[:, 0:Q], ACT.Abs, bias=neg_centre[:, c : c + 1])
+                nc.tensor.matmul(
+                    neg_margin[:, c * P : (c + 1) * P],
+                    lhsT=dist[:],
+                    rhs=ident[:],
+                    is_transpose=True,
+                    start=False,
+                    stop=(c == 1),
+                )
+            running = sb.tile([P, 1], F32, name="neg_max%d" % h)
+            nc.vector.tensor_scalar(
+                out=neg_s[:, h * HALF : (h + 1) * HALF],
+                in0=neg_margin[:, 0:HALF],
+                scalar1=lam_sb[:],
+                scalar2=neg_max[-1][:] if neg_max else None,
+                op0=ALU.mult,
+                op1=ALU.min,
+                accum_out=running[:],
+            )
+            neg_max.append(running)
+
+        p_sb = sb.tile([P, I], F32, name="p_sb")
+        row_sum = sb.tile([P, 1], F32, name="row_sum")
+        nc.scalar.activation(p_sb[:], neg_s[:], ACT.Exp, bias=neg_max[-1][:], scale=-1.0, accum_out=row_sum[:])
+        inv_sum = sb.tile([P, 1], F32, name="inv_sum")
+        nc.vector.reciprocal(inv_sum[:], row_sum[:])
+
+        shares = []
+        group_sums = []
+        for h in range(2):
+            share = sb.tile([P, HALF], F32, name="share%d" % h)
+            nc.vector.tensor_scalar(
+                out=share[:], in0=p_sb[:, h * HALF : (h + 1) * HALF], scalar1=inv_sum[:], scalar2=128.0 * 128.0, op0=ALU.mult, op1=ALU.mult
+            )
+            shares.append(share)
+        for h in range(2):
+            share_t = bank(h, "share_t%d" % h)
+            for c in range(2):
+                nc.tensor.transpose(share_t[:, c * P : (c + 1) * P], shares[h][:, c * P : (c + 1) * P], ident[:])
+            group_sum = sb.tile([P, 2 * K], F32, name="group_sum%d" % h)
+            nc.vector.tensor_reduce(group_sum[:], share_t[:, 0:HALF].rearrange("p (g j) -> p g j", j=GROUP), AX.X, ALU.add)
+            group_sums.append(group_sum)
+        factors_t = []
+        for h in range(2):
+            factor_t = sb.tile([P, 2 * K, GROUP], F32, name="factor_t%d" % h)
+            nc.scalar.activation(
+                factor_t[:], group_sums[h][:].unsqueeze(2).to_broadcast([P, 2 * K, GROUP]), ACT.Abs_reciprocal_sqrt, bias=1e-30
+            )
+            factors_t.append(factor_t)
+        for h in range(2):
+            factor_ps = bank(2 + h, "factor_ps%d" % h)
+            flat = factors_t[h][:].rearrange("p g j -> p (g j)")
+            for c in range(2):
+                nc.tensor.transpose(factor_ps[:, c * P : (c + 1) * P], flat[:, c * P : (c + 1) * P], ident[:])
+            factor = sb.tile([P, HALF], F32, name="factor%d" % h)
+            nc.scalar.copy(factor[:], factor_ps[:, 0:HALF])
+            nc.vector.tensor_tensor(placed[:].indirect(half_of(offs2_sb, h)), shares[h][:], factor[:], ALU.mult)
+
+        col = 0
+        for n, width in enumerate(OUT_COLS):
+            result = sb.tile([P, width], F32, name="result%d" % n)
+            nc.vector.scalar_tensor_tensor(
+                out=result[:], in0=old_sb[:, col : col + width], scalar=fade_sb[:], in1=placed[:, col : col + width], op0=ALU.mult, op1=ALU.add
+            )
+            nc.sync.dma_start(out=out[:, col : col + width], in_=result[:])
+            col += width

@@ -39,23 +39,25 @@ def tile_attend_interval_balanced_counts_kernel(tc, query, keys_words, keys_scal
 
         offs_sb = sb.tile([P, I // 16], U16, name="offs_sb")
         offs2_sb = sb.tile([P, I // 16], U16, name="offs2_sb")
-        scale_win = sb.tile([P, T], U8, name="scale_win")
-        word_win = sb.tile([P, T], U16, name="word_win")
-        low_win = sb.tile([P, T], F32, name="low_win", tag="low_then_old")
-        high_win = sb.tile([P, T], F32, name="high_win", tag="high_then_fade")
+        scale_win = sb.tile([P, T], U8, name="scale_win", tag="scales_then_placed")
+        word_win = sb.tile([P, T], U16, name="word_win", tag="words_then_old")
+        low_win = sb.tile([P, T], F32, name="low_win")
+        high_win = sb.tile([P, T], F32, name="high_win")
         q_raw = sb.tile([P, PACK, Q], F32, name="q_raw", tag="query_then_lam")
         ident = sb.tile([P, P], F32, name="ident")
 
         nc.vector.memset(scale_win[:].bitcast(I32), 0)
         nc.vector.memset(low_win[0:ROW, :], 0.0)
         nc.vector.memset(high_win[0:ROW, :], 0.0)
+        one = sb.tile([P, 1], F32, name="one")
+        nc.gpsimd.memset(one[:], 1.0)
         make_identity(nc, ident[:])
 
         nc.sync.dma_start(offs_sb[:], offs)
-        nc.sync.dma_start(out=q_raw[:], in_=query.rearrange("(p j) q -> p j q", j=PACK))
-        nc.sync.dma_start(out=word_win[:].bitcast(I32), in_=keys_words[0].bitcast(I32))
         nc.scalar.dma_start(out=low_win[ROW:P, :], in_=lowend[0:1, :])
         nc.scalar.dma_start(out=high_win[ROW:P, :], in_=highend[0:1, :])
+        nc.sync.dma_start(out=word_win[:].bitcast(I32), in_=keys_words[0].bitcast(I32))
+        nc.sync.dma_start(out=q_raw[:], in_=query.rearrange("(p j) q -> p j q", j=PACK))
         for quad in range(4):
             nc.sync.dma_start(
                 out=scale_win[32 * quad : 32 * quad + 4, :].bitcast(I32),
@@ -66,65 +68,53 @@ def tile_attend_interval_balanced_counts_kernel(tc, query, keys_words, keys_scal
         def half_of(list_tile, h):
             return list_tile[:, h * (HALF // 16) : (h + 1) * (HALF // 16)]
 
-        q_bf = sb.tile([P, Q, PACK], BF16, name="q_bf", tag="q_bf_then_counts", align_bytes=64)
+        guard = sb.tile([P, 1], F32, name="guard")
+        nc.scalar.activation(guard[:], one[:], ACT.Copy, scale=1e-30)
+
+        low = sb.tile([P, I], F32, name="low")
+        nc.scalar.activation(low[:], low_win[:].indirect(offs_sb[:]), ACT.Copy)
+
+        q_bf = sb.tile([P, Q, PACK], BF16, name="q_bf", tag="q_bf_then_fade", align_bytes=64)
         q_codes = sb.tile([P, Q], U32, name="q_codes", align_bytes=64)
         q_scales = sb.tile([P, Q], U8, name="q_scales", align_bytes=64)
         nc.scalar.copy(q_bf[:], q_raw[:].rearrange("p j q -> p q j"))
         lam_sb = sb.tile([P, 1], F32, name="lam_sb", tag="query_then_lam")
         nc.sync.dma_start(out=lam_sb[:], in_=lam)
 
-        lows = [sb.tile([P, HALF], F32, name="low%d" % h) for h in range(2)]
         highs = [sb.tile([P, HALF], F32, name="high%d" % h) for h in range(2)]
-        nc.vector.tensor_copy(lows[0][:], low_win[:].indirect(half_of(offs_sb, 0)))
-        nc.scalar.activation(highs[0][:], high_win[:].indirect(half_of(offs_sb, 0)), ACT.Copy)
-        nc.scalar.activation(lows[1][:], low_win[:].indirect(half_of(offs_sb, 1)), ACT.Copy)
-        nc.scalar.activation(highs[1][:], high_win[:].indirect(half_of(offs_sb, 1)), ACT.Copy)
-        old_sb = sb.tile([P, M], F32, name="old_sb", tag="low_then_old")
-        nc.sync.dma_start(out=old_sb[:], in_=old)
-        fade_sb = sb.tile([P, 1], F32, name="fade_sb", tag="high_then_fade")
-        nc.sync.dma_start(out=fade_sb[:], in_=fade)
-
-        nc.vector.quantize_mx(out=q_codes[:].bitcast(FP8X4), scales=q_scales[:], in_=q_bf[:].rearrange("p q j -> p (q j)"))
-        words = []
-        scales = []
+        words = [sb.tile([P, HALF], U16, name="key_words%d" % h, align_bytes=64) for h in range(2)]
+        scales = [sb.tile([P, HALF], U8, name="key_scales%d" % h, align_bytes=64) for h in range(2)]
         for h in range(2):
-            key_words = sb.tile([P, HALF], U16, name="key_words%d" % h, align_bytes=64)
-            nc.vector.tensor_copy(key_words[:], word_win[:].indirect(half_of(offs_sb, h)))
-            words.append(key_words)
-            key_scales = sb.tile([P, HALF], U8, name="key_scales%d" % h, align_bytes=64)
-            nc.vector.tensor_copy(key_scales[:], scale_win[:].indirect(half_of(offs_sb, h)))
-            scales.append(key_scales)
+            nc.scalar.activation(highs[h][:], high_win[:].indirect(half_of(offs_sb, h)), ACT.Copy)
+            nc.vector.tensor_copy(words[h][:], word_win[:].indirect(half_of(offs_sb, h)))
+        nc.vector.tensor_copy(scales[0][:], scale_win[:].indirect(half_of(offs_sb, 0)))
+        nc.vector.quantize_mx(out=q_codes[:].bitcast(FP8X4), scales=q_scales[:], in_=q_bf[:].rearrange("p q j -> p (q j)"))
+        nc.vector.tensor_copy(scales[1][:], scale_win[:].indirect(half_of(offs_sb, 1)))
 
-        placed = sb.tile([P, M], F32, name="placed", tag="q_bf_then_counts", align_bytes=64)
+        old_sb = sb.tile([P, M], F32, name="old_sb", tag="words_then_old")
+        nc.sync.dma_start(out=old_sb[:], in_=old)
+        fade_sb = sb.tile([P, 1], F32, name="fade_sb", tag="q_bf_then_fade", align_bytes=64)
+        nc.sync.dma_start(out=fade_sb[:], in_=fade)
+        placed = sb.tile([P, M], F32, name="placed", tag="scales_then_placed")
         nc.gpsimd.memset(placed[:], 0.0)
+
+        low_t = bank(0, "low_t")
+        high_t = bank(1, "high_t")
+        for chunk in range(4):
+            nc.tensor.transpose(low_t[:, chunk * P : (chunk + 1) * P], low[:, chunk * P : (chunk + 1) * P], ident[:])
+        for chunk in range(4):
+            c = chunk % 2
+            nc.tensor.transpose(high_t[:, chunk * P : (chunk + 1) * P], highs[chunk // 2][:, c * P : (c + 1) * P], ident[:])
+        low_col = sb.tile([P, 4], F32, name="low_col")
+        nc.scalar.copy(low_col[:], low_t[:, ROW::P])
 
         neg_s = sb.tile([P, I], F32, name="neg_s")
         neg_max = []
         for h in range(2):
-            ends_t = bank(h, "ends_t%d" % h)
-            for c in range(2):
-                nc.tensor.transpose(ends_t[:, c * P : (c + 1) * P], lows[h][:, c * P : (c + 1) * P], ident[:])
-            for c in range(2):
-                nc.tensor.transpose(ends_t[:, (2 + c) * P : (3 + c) * P], highs[h][:, c * P : (c + 1) * P], ident[:])
-            neg_half_ends = sb.tile([P, 4], F32, name="neg_half_ends%d" % h)
-            nc.scalar.activation(neg_half_ends[:], ends_t[:, ROW::P], ACT.Copy, scale=-0.5)
-            neg_centre = sb.tile([P, 2], F32, name="neg_centre%d" % h)
-            neg_radius = sb.tile([P, 2], F32, name="neg_radius%d" % h)
-            nc.vector.tensor_tensor(neg_centre[:], neg_half_ends[:, 2:4], neg_half_ends[:, 0:2], ALU.add)
-            nc.vector.tensor_tensor(neg_radius[:], neg_half_ends[:, 2:4], neg_half_ends[:, 0:2], ALU.subtract)
-
             neg_margin = bank(6 + h, "neg_margin%d" % h)
             for c in range(2):
-                nc.tensor.matmul(
-                    neg_margin[:, c * P : (c + 1) * P],
-                    lhsT=neg_radius[:, c : c + 1].to_broadcast([P, P]),
-                    rhs=ident[:],
-                    is_transpose=True,
-                    start=(c == 0),
-                    stop=False,
-                )
-            for c in range(2):
-                prod = bank(2 + 2 * h + c, "prod%d%d" % (h, c))
+                chunk = 2 * h + c
+                prod = bank(2 + chunk, "prod%d" % chunk)
                 nc.tensor.matmul_mx(
                     out=prod[:, 0:Q],
                     lhsT=words[h][:, c * P : (c + 1) * P].bitcast(FP4X4),
@@ -134,16 +124,14 @@ def tile_attend_interval_balanced_counts_kernel(tc, query, keys_words, keys_scal
                     start=True,
                     stop=True,
                 )
-                dist = sb.tile([P, Q], F32, name="dist%d%d" % (h, c))
-                nc.scalar.activation(dist[:], prod[:, 0:Q], ACT.Abs, bias=neg_centre[:, c : c + 1])
-                nc.tensor.matmul(
-                    neg_margin[:, c * P : (c + 1) * P],
-                    lhsT=dist[:],
-                    rhs=ident[:],
-                    is_transpose=True,
-                    start=False,
-                    stop=(c == 1),
+                below = sb.tile([P, Q], F32, name="below%d" % chunk)
+                nc.scalar.activation(below[:], prod[:, 0:Q], ACT.Identity, bias=low_col[:, chunk : chunk + 1], scale=-1.0)
+                outside = sb.tile([P, Q], F32, name="outside%d" % chunk)
+                high_col = chunk * P + ROW
+                nc.vector.scalar_tensor_tensor(
+                    out=outside[:], in0=prod[:, 0:Q], scalar=high_t[:, high_col : high_col + 1], in1=below[:], op0=ALU.subtract, op1=ALU.max
                 )
+                nc.tensor.transpose(neg_margin[:, c * P : (c + 1) * P], outside[:], ident[:])
             running = sb.tile([P, 1], F32, name="neg_max%d" % h)
             nc.vector.tensor_scalar(
                 out=neg_s[:, h * HALF : (h + 1) * HALF],
@@ -163,35 +151,41 @@ def tile_attend_interval_balanced_counts_kernel(tc, query, keys_words, keys_scal
         nc.vector.reciprocal(inv_sum[:], row_sum[:])
 
         shares = []
-        group_sums = []
         for h in range(2):
-            share = sb.tile([P, HALF], F32, name="share%d" % h)
+            share = sb.tile([P, HALF], F32, name="share%d" % h, align_bytes=64)
             nc.vector.tensor_scalar(
                 out=share[:], in0=p_sb[:, h * HALF : (h + 1) * HALF], scalar1=inv_sum[:], scalar2=128.0 * 128.0, op0=ALU.mult, op1=ALU.mult
             )
             shares.append(share)
-        for h in range(2):
-            share_t = bank(h, "share_t%d" % h)
-            for c in range(2):
-                nc.tensor.transpose(share_t[:, c * P : (c + 1) * P], shares[h][:, c * P : (c + 1) * P], ident[:])
-            group_sum = sb.tile([P, 2 * K], F32, name="group_sum%d" % h)
-            nc.vector.tensor_reduce(group_sum[:], share_t[:, 0:HALF].rearrange("p (g j) -> p g j", j=GROUP), AX.X, ALU.add)
-            group_sums.append(group_sum)
-        factors_t = []
-        for h in range(2):
-            factor_t = sb.tile([P, 2 * K, GROUP], F32, name="factor_t%d" % h)
+
+        def group_factors(share_t, h):
+            group_sum = sb.tile([P, HALF // GROUP], F32, name="group_sum%d" % h)
+            nc.vector.tensor_reduce(group_sum[:], share_t.rearrange("p (g j) -> p g j", j=GROUP), AX.X, ALU.add)
+            factor_t = sb.tile([P, HALF], F32, name="factor_t%d" % h, align_bytes=64)
             nc.scalar.activation(
-                factor_t[:], group_sums[h][:].unsqueeze(2).to_broadcast([P, 2 * K, GROUP]), ACT.Abs_reciprocal_sqrt, bias=1e-30
+                factor_t[:].rearrange("p (g j) -> p g j", j=GROUP),
+                group_sum[:].unsqueeze(2).to_broadcast([P, HALF // GROUP, GROUP]),
+                ACT.Abs_reciprocal_sqrt,
+                bias=guard[:],
             )
-            factors_t.append(factor_t)
+            return factor_t
+
+        share_ps = bank(0, "share_ps")
+        for c in range(2):
+            nc.tensor.transpose(share_ps[:, c * P : (c + 1) * P], shares[1][:, c * P : (c + 1) * P], ident[:])
+        share_blocks = sb.tile([P, HALF], F32, name="share_blocks", align_bytes=64)
+        nc.vector.transpose(share_blocks[:], shares[0][:])
+        factor_blocks = group_factors(share_blocks[:], 0)
+        factor_t = group_factors(share_ps[:, 0:HALF], 1)
+
+        factors = [sb.tile([P, HALF], F32, name="factor%d" % h, align_bytes=64) for h in range(2)]
+        nc.vector.transpose(factors[0][:], factor_blocks[:])
+        factor_ps = bank(2, "factor_ps")
+        for c in range(2):
+            nc.tensor.transpose(factor_ps[:, c * P : (c + 1) * P], factor_t[:, c * P : (c + 1) * P], ident[:])
+        nc.scalar.copy(factors[1][:], factor_ps[:, 0:HALF])
         for h in range(2):
-            factor_ps = bank(2 + h, "factor_ps%d" % h)
-            flat = factors_t[h][:].rearrange("p g j -> p (g j)")
-            for c in range(2):
-                nc.tensor.transpose(factor_ps[:, c * P : (c + 1) * P], flat[:, c * P : (c + 1) * P], ident[:])
-            factor = sb.tile([P, HALF], F32, name="factor%d" % h)
-            nc.scalar.copy(factor[:], factor_ps[:, 0:HALF])
-            nc.vector.tensor_tensor(placed[:].indirect(half_of(offs2_sb, h)), shares[h][:], factor[:], ALU.mult)
+            nc.vector.tensor_tensor(placed[:].indirect(half_of(offs2_sb, h)), shares[h][:], factors[h][:], ALU.mult)
 
         col = 0
         for n, width in enumerate(OUT_COLS):

@@ -22,7 +22,7 @@ PACK = 4
 HALF = I // 2
 GROUP = Q // K
 ROW = P - 1
-OUT_COLS = [256, 512, 512, 512, 256]
+OUT_COLS = [384, 512, 512, 512, 128]
 
 FLOPS = 2 * D * Q * I
 BYTES = 4 * D * Q + 2 * P * T + 16 * T + 2 * 4 * T + 2 * 4 * Q + 2 * 4 * Q * M + 2 * 2 * P * (I // 16)
@@ -32,6 +32,7 @@ def tile_attend_interval_balanced_counts_kernel(tc, query, keys_words, keys_scal
     nc = tc.nc
     with ExitStack() as ctx:
         sb = ctx.enter_context(tc.tile_pool(name="sb", bufs=1))
+        keys_pool = ctx.enter_context(tc.tile_pool(name="keys_pool", bufs=1))
         ps = ctx.enter_context(tc.psum_pool(name="ps", bufs=1))
 
         def bank(n, name):
@@ -40,23 +41,23 @@ def tile_attend_interval_balanced_counts_kernel(tc, query, keys_words, keys_scal
         offs_sb = sb.tile([P, I // 16], U16, name="offs_sb")
         offs2_sb = sb.tile([P, I // 16], U16, name="offs2_sb")
         scale_win = sb.tile([P, T], U8, name="scale_win", tag="scales_then_placed")
-        word_win = sb.tile([P, T], U16, name="word_win", tag="words_then_old")
-        low_win = sb.tile([P, T], F32, name="low_win")
-        high_win = sb.tile([P, T], F32, name="high_win")
-        q_raw = sb.tile([P, PACK, Q], F32, name="q_raw", tag="query_then_lam")
+        word_win = keys_pool.tile([P, T], U16, name="word_win", offset=0)
+        low_win = sb.tile([P, T], F32, name="low_win", tag="low_then_lam")
+        high_win = sb.tile([P, T], F32, name="high_win", tag="high_then_fade", align_bytes=64)
+        q_raw = sb.tile([P, PACK, Q], F32, name="q_raw", tag="query_then_old")
         ident = sb.tile([P, P], F32, name="ident")
 
         nc.vector.memset(scale_win[:].bitcast(I32), 0)
         nc.vector.memset(low_win[0:ROW, :], 0.0)
-        nc.vector.memset(high_win[0:ROW, :], 0.0)
         one = sb.tile([P, 1], F32, name="one")
         nc.gpsimd.memset(one[:], 1.0)
         make_identity(nc, ident[:])
+        nc.gpsimd.memset(high_win[0:ROW, :], 0.0)
 
         nc.sync.dma_start(offs_sb[:], offs)
-        nc.scalar.dma_start(out=low_win[ROW:P, :], in_=lowend[0:1, :])
-        nc.scalar.dma_start(out=high_win[ROW:P, :], in_=highend[0:1, :])
+        nc.sync.dma_start(out=low_win[ROW:P, :], in_=lowend[0:1, :])
         nc.sync.dma_start(out=word_win[:].bitcast(I32), in_=keys_words[0].bitcast(I32))
+        nc.sync.dma_start(out=high_win[ROW:P, :], in_=highend[0:1, :])
         nc.sync.dma_start(out=q_raw[:], in_=query.rearrange("(p j) q -> p j q", j=PACK))
         for quad in range(4):
             nc.sync.dma_start(
@@ -71,29 +72,29 @@ def tile_attend_interval_balanced_counts_kernel(tc, query, keys_words, keys_scal
         guard = sb.tile([P, 1], F32, name="guard")
         nc.scalar.activation(guard[:], one[:], ACT.Copy, scale=1e-30)
 
-        low = sb.tile([P, I], F32, name="low")
-        nc.scalar.activation(low[:], low_win[:].indirect(offs_sb[:]), ACT.Copy)
-
-        q_bf = sb.tile([P, Q, PACK], BF16, name="q_bf", tag="q_bf_then_fade", align_bytes=64)
-        q_codes = sb.tile([P, Q], U32, name="q_codes", align_bytes=64)
-        q_scales = sb.tile([P, Q], U8, name="q_scales", align_bytes=64)
-        nc.scalar.copy(q_bf[:], q_raw[:].rearrange("p j q -> p q j"))
-        lam_sb = sb.tile([P, 1], F32, name="lam_sb", tag="query_then_lam")
+        lows = [sb.tile([P, HALF], F32, name="low%d" % h) for h in range(2)]
+        high = sb.tile([P, I], F32, name="high")
+        nc.vector.tensor_copy(lows[0][:], low_win[:].indirect(half_of(offs_sb, 0)))
+        nc.scalar.activation(lows[1][:], low_win[:].indirect(half_of(offs_sb, 1)), ACT.Copy)
+        nc.scalar.activation(high[:], high_win[:].indirect(offs_sb[:]), ACT.Copy)
+        lam_sb = sb.tile([P, 1], F32, name="lam_sb", tag="low_then_lam")
         nc.sync.dma_start(out=lam_sb[:], in_=lam)
 
-        highs = [sb.tile([P, HALF], F32, name="high%d" % h) for h in range(2)]
-        words = [sb.tile([P, HALF], U16, name="key_words%d" % h, align_bytes=64) for h in range(2)]
-        scales = [sb.tile([P, HALF], U8, name="key_scales%d" % h, align_bytes=64) for h in range(2)]
-        for h in range(2):
-            nc.scalar.activation(highs[h][:], high_win[:].indirect(half_of(offs_sb, h)), ACT.Copy)
-            nc.vector.tensor_copy(words[h][:], word_win[:].indirect(half_of(offs_sb, h)))
-        nc.vector.tensor_copy(scales[0][:], scale_win[:].indirect(half_of(offs_sb, 0)))
-        nc.vector.quantize_mx(out=q_codes[:].bitcast(FP8X4), scales=q_scales[:], in_=q_bf[:].rearrange("p q j -> p (q j)"))
-        nc.vector.tensor_copy(scales[1][:], scale_win[:].indirect(half_of(offs_sb, 1)))
+        q_bf = sb.tile([P, Q, PACK], BF16, name="q_bf", align_bytes=64)
+        nc.gpsimd.tensor_scalar(out=q_bf[:], in0=q_raw[:].rearrange("p j q -> p q j"), scalar1=1.0, scalar2=0.0, op0=ALU.mult, op1=ALU.add)
 
-        old_sb = sb.tile([P, M], F32, name="old_sb", tag="words_then_old")
+        words = sb.tile([P, I], U16, name="key_words", align_bytes=64)
+        nc.vector.tensor_copy(words[:], word_win[:].indirect(offs_sb[:]))
+        scales = [keys_pool.tile([P, HALF], U8, name="key_scales%d" % h, align_bytes=64, offset=h * HALF) for h in range(2)]
+        q_codes = keys_pool.tile([P, Q], U32, name="q_codes", align_bytes=64, offset=I)
+        q_scales = sb.tile([P, Q], U8, name="q_scales", align_bytes=64)
+        nc.vector.quantize_mx(out=q_codes[:].bitcast(FP8X4), scales=q_scales[:], in_=q_bf[:].rearrange("p q j -> p (q j)"))
+        for h in range(2):
+            nc.vector.tensor_copy(scales[h][:], scale_win[:].indirect(half_of(offs_sb, h)))
+
+        old_sb = sb.tile([P, M], F32, name="old_sb", tag="query_then_old")
         nc.sync.dma_start(out=old_sb[:], in_=old)
-        fade_sb = sb.tile([P, 1], F32, name="fade_sb", tag="q_bf_then_fade", align_bytes=64)
+        fade_sb = sb.tile([P, 1], F32, name="fade_sb", tag="high_then_fade", align_bytes=64)
         nc.sync.dma_start(out=fade_sb[:], in_=fade)
         placed = sb.tile([P, M], F32, name="placed", tag="scales_then_placed")
         nc.gpsimd.memset(placed[:], 0.0)
@@ -101,23 +102,22 @@ def tile_attend_interval_balanced_counts_kernel(tc, query, keys_words, keys_scal
         low_t = bank(0, "low_t")
         high_t = bank(1, "high_t")
         for chunk in range(4):
-            nc.tensor.transpose(low_t[:, chunk * P : (chunk + 1) * P], low[:, chunk * P : (chunk + 1) * P], ident[:])
-        for chunk in range(4):
             c = chunk % 2
-            nc.tensor.transpose(high_t[:, chunk * P : (chunk + 1) * P], highs[chunk // 2][:, c * P : (c + 1) * P], ident[:])
+            nc.tensor.transpose(low_t[:, chunk * P : (chunk + 1) * P], lows[chunk // 2][:, c * P : (c + 1) * P], ident[:])
+        for chunk in range(4):
+            nc.tensor.transpose(high_t[:, chunk * P : (chunk + 1) * P], high[:, chunk * P : (chunk + 1) * P], ident[:])
         low_col = sb.tile([P, 4], F32, name="low_col")
         nc.scalar.copy(low_col[:], low_t[:, ROW::P])
 
         neg_s = sb.tile([P, I], F32, name="neg_s")
-        neg_max = []
+        neg_margin = bank(6, "neg_margin")
         for h in range(2):
-            neg_margin = bank(6 + h, "neg_margin%d" % h)
             for c in range(2):
                 chunk = 2 * h + c
                 prod = bank(2 + chunk, "prod%d" % chunk)
                 nc.tensor.matmul_mx(
                     out=prod[:, 0:Q],
-                    lhsT=words[h][:, c * P : (c + 1) * P].bitcast(FP4X4),
+                    lhsT=words[:, chunk * P : (chunk + 1) * P].bitcast(FP4X4),
                     lhsT_scale=scales[h][:, c * P : (c + 1) * P],
                     rhs=q_codes[:].bitcast(FP8X4),
                     rhs_scale=q_scales[:],
@@ -131,22 +131,15 @@ def tile_attend_interval_balanced_counts_kernel(tc, query, keys_words, keys_scal
                 nc.vector.scalar_tensor_tensor(
                     out=outside[:], in0=prod[:, 0:Q], scalar=high_t[:, high_col : high_col + 1], in1=below[:], op0=ALU.subtract, op1=ALU.max
                 )
-                nc.tensor.transpose(neg_margin[:, c * P : (c + 1) * P], outside[:], ident[:])
-            running = sb.tile([P, 1], F32, name="neg_max%d" % h)
-            nc.vector.tensor_scalar(
-                out=neg_s[:, h * HALF : (h + 1) * HALF],
-                in0=neg_margin[:, 0:HALF],
-                scalar1=lam_sb[:],
-                scalar2=neg_max[-1][:] if neg_max else None,
-                op0=ALU.mult,
-                op1=ALU.min,
-                accum_out=running[:],
-            )
-            neg_max.append(running)
+                nc.tensor.transpose(neg_margin[:, chunk * P : (chunk + 1) * P], outside[:], ident[:])
+        neg_max = sb.tile([P, 1], F32, name="neg_max")
+        nc.vector.tensor_scalar(
+            out=neg_s[:], in0=neg_margin[:], scalar1=lam_sb[:], scalar2=None, op0=ALU.mult, op1=ALU.min, accum_out=neg_max[:]
+        )
 
         p_sb = sb.tile([P, I], F32, name="p_sb")
         row_sum = sb.tile([P, 1], F32, name="row_sum")
-        nc.scalar.activation(p_sb[:], neg_s[:], ACT.Exp, bias=neg_max[-1][:], scale=-1.0, accum_out=row_sum[:])
+        nc.scalar.activation(p_sb[:], neg_s[:], ACT.Exp, bias=neg_max[:], scale=-1.0, accum_out=row_sum[:])
         inv_sum = sb.tile([P, 1], F32, name="inv_sum")
         nc.vector.reciprocal(inv_sum[:], row_sum[:])
 

@@ -19,13 +19,18 @@ AX = mybir.AxisListType
 
 P = 128
 PACK = 4
+CHUNKS = I // P
 HALF = I // 2
 GROUP = Q // K
 ROW = P - 1
+BANK = 512
+SCALE_ROWS = 4
 OUT_COLS = [384, 512, 512, 512, 128]
+SHARE_SCALE = 128.0 * 128.0
+TINY = 1e-30
 
 FLOPS = 2 * D * Q * I
-BYTES = 4 * D * Q + 2 * P * T + 16 * T + 2 * 4 * T + 2 * 4 * Q + 2 * 4 * Q * M + 2 * 2 * P * (I // 16)
+BYTES = 4 * D * Q + 2 * P * T + (D // 32) * T + 2 * 4 * T + 2 * 4 * Q + 2 * 4 * Q * M + 2 * 2 * P * (I // 16)
 
 
 def tile_attend_interval_balanced_counts_kernel(tc, query, keys_words, keys_scales, lowend, highend, lam, old, fade, offs, offs2, out):
@@ -33,60 +38,64 @@ def tile_attend_interval_balanced_counts_kernel(tc, query, keys_words, keys_scal
     with ExitStack() as ctx:
         sb = ctx.enter_context(tc.tile_pool(name="sb", bufs=1))
         keys_pool = ctx.enter_context(tc.tile_pool(name="keys_pool", bufs=1))
+        high_pool = ctx.enter_context(tc.tile_pool(name="high_pool", bufs=1))
         ps = ctx.enter_context(tc.psum_pool(name="ps", bufs=1))
 
         def bank(n, name):
-            return ps.tile([P, 512], F32, name=name, tag="bank%d" % n)
+            return ps.tile([P, BANK], F32, name=name, tag="bank%d" % n)
+
+        def half_of(list_tile, h):
+            return list_tile[:, h * (HALF // 16) : (h + 1) * (HALF // 16)]
+
+        def cols(chunk):
+            return slice(chunk * P, (chunk + 1) * P)
 
         offs_sb = sb.tile([P, I // 16], U16, name="offs_sb")
         offs2_sb = sb.tile([P, I // 16], U16, name="offs2_sb")
         scale_win = sb.tile([P, T], U8, name="scale_win", tag="scales_then_placed")
         word_win = keys_pool.tile([P, T], U16, name="word_win", offset=0)
         low_win = sb.tile([P, T], F32, name="low_win", tag="low_then_lam")
-        high_win = sb.tile([P, T], F32, name="high_win", tag="high_then_fade", align_bytes=64)
+        high_win = high_pool.tile([P, T], F32, name="high_win", offset=0)
         q_raw = sb.tile([P, PACK, Q], F32, name="q_raw", tag="query_then_old")
         ident = sb.tile([P, P], F32, name="ident")
 
         nc.vector.memset(scale_win[:].bitcast(I32), 0)
+        nc.vector.memset(high_win[0:ROW, :], 0.0)
         nc.vector.memset(low_win[0:ROW, :], 0.0)
         one = sb.tile([P, 1], F32, name="one")
         nc.gpsimd.memset(one[:], 1.0)
         make_identity(nc, ident[:])
-        nc.gpsimd.memset(high_win[0:ROW, :], 0.0)
 
         nc.sync.dma_start(offs_sb[:], offs)
+        nc.sync.dma_start(out=high_win[ROW:P, :], in_=highend[0:1, :])
         nc.sync.dma_start(out=low_win[ROW:P, :], in_=lowend[0:1, :])
         nc.sync.dma_start(out=word_win[:].bitcast(I32), in_=keys_words[0].bitcast(I32))
-        nc.sync.dma_start(out=high_win[ROW:P, :], in_=highend[0:1, :])
         nc.sync.dma_start(out=q_raw[:], in_=query.rearrange("(p j) q -> p j q", j=PACK))
-        for quad in range(4):
+        for quad in range(P // 32):
             nc.sync.dma_start(
-                out=scale_win[32 * quad : 32 * quad + 4, :].bitcast(I32),
-                in_=keys_scales[0, 4 * quad : 4 * quad + 4, :].bitcast(I32),
+                out=scale_win[32 * quad : 32 * quad + SCALE_ROWS, :].bitcast(I32),
+                in_=keys_scales[0, SCALE_ROWS * quad : SCALE_ROWS * (quad + 1), :].bitcast(I32),
             )
         nc.sync.dma_start(offs2_sb[:], offs2)
 
-        def half_of(list_tile, h):
-            return list_tile[:, h * (HALF // 16) : (h + 1) * (HALF // 16)]
-
         guard = sb.tile([P, 1], F32, name="guard")
-        nc.scalar.activation(guard[:], one[:], ACT.Copy, scale=1e-30)
+        nc.scalar.activation(guard[:], one[:], ACT.Copy, scale=TINY)
 
         lows = [sb.tile([P, HALF], F32, name="low%d" % h) for h in range(2)]
         high = sb.tile([P, I], F32, name="high")
+        nc.scalar.activation(high[:], high_win[:].indirect(offs_sb[:]), ACT.Copy)
         nc.vector.tensor_copy(lows[0][:], low_win[:].indirect(half_of(offs_sb, 0)))
         nc.scalar.activation(lows[1][:], low_win[:].indirect(half_of(offs_sb, 1)), ACT.Copy)
-        nc.scalar.activation(high[:], high_win[:].indirect(offs_sb[:]), ACT.Copy)
         lam_sb = sb.tile([P, 1], F32, name="lam_sb", tag="low_then_lam")
         nc.sync.dma_start(out=lam_sb[:], in_=lam)
 
-        q_bf = sb.tile([P, Q, PACK], BF16, name="q_bf", align_bytes=64)
-        nc.gpsimd.tensor_scalar(out=q_bf[:], in0=q_raw[:].rearrange("p j q -> p q j"), scalar1=1.0, scalar2=0.0, op0=ALU.mult, op1=ALU.add)
+        q_bf = high_pool.tile([P, Q, PACK], BF16, name="q_bf", align_bytes=64, offset=0)
+        nc.scalar.copy(q_bf[:], q_raw[:].rearrange("p j q -> p q j"))
 
         words = sb.tile([P, I], U16, name="key_words", align_bytes=64)
         nc.vector.tensor_copy(words[:], word_win[:].indirect(offs_sb[:]))
-        scales = [keys_pool.tile([P, HALF], U8, name="key_scales%d" % h, align_bytes=64, offset=h * HALF) for h in range(2)]
-        q_codes = keys_pool.tile([P, Q], U32, name="q_codes", align_bytes=64, offset=I)
+        scales = [high_pool.tile([P, HALF], U8, name="key_scales%d" % h, align_bytes=64, offset=h * HALF) for h in range(2)]
+        q_codes = keys_pool.tile([P, Q], U32, name="q_codes", align_bytes=64, offset=0)
         q_scales = sb.tile([P, Q], U8, name="q_scales", align_bytes=64)
         nc.vector.quantize_mx(out=q_codes[:].bitcast(FP8X4), scales=q_scales[:], in_=q_bf[:].rearrange("p q j -> p (q j)"))
         for h in range(2):
@@ -94,78 +103,74 @@ def tile_attend_interval_balanced_counts_kernel(tc, query, keys_words, keys_scal
 
         old_sb = sb.tile([P, M], F32, name="old_sb", tag="query_then_old")
         nc.sync.dma_start(out=old_sb[:], in_=old)
-        fade_sb = sb.tile([P, 1], F32, name="fade_sb", tag="high_then_fade", align_bytes=64)
+        fade_sb = keys_pool.tile([P, 1], F32, name="fade_sb", offset=4 * Q)
         nc.sync.dma_start(out=fade_sb[:], in_=fade)
         placed = sb.tile([P, M], F32, name="placed", tag="scales_then_placed")
         nc.gpsimd.memset(placed[:], 0.0)
 
         low_t = bank(0, "low_t")
         high_t = bank(1, "high_t")
-        for chunk in range(4):
-            c = chunk % 2
-            nc.tensor.transpose(low_t[:, chunk * P : (chunk + 1) * P], lows[chunk // 2][:, c * P : (c + 1) * P], ident[:])
-        for chunk in range(4):
-            nc.tensor.transpose(high_t[:, chunk * P : (chunk + 1) * P], high[:, chunk * P : (chunk + 1) * P], ident[:])
-        low_col = sb.tile([P, 4], F32, name="low_col")
+        for chunk in range(CHUNKS):
+            nc.tensor.transpose(high_t[:, cols(chunk)], high[:, cols(chunk)], ident[:])
+        for chunk in range(CHUNKS):
+            nc.tensor.transpose(low_t[:, cols(chunk)], lows[chunk // 2][:, cols(chunk % 2)], ident[:])
+        low_col = sb.tile([P, CHUNKS], F32, name="low_col")
         nc.scalar.copy(low_col[:], low_t[:, ROW::P])
 
-        neg_s = sb.tile([P, I], F32, name="neg_s")
         neg_margin = bank(6, "neg_margin")
-        for h in range(2):
-            for c in range(2):
-                chunk = 2 * h + c
-                prod = bank(2 + chunk, "prod%d" % chunk)
-                nc.tensor.matmul_mx(
-                    out=prod[:, 0:Q],
-                    lhsT=words[:, chunk * P : (chunk + 1) * P].bitcast(FP4X4),
-                    lhsT_scale=scales[h][:, c * P : (c + 1) * P],
-                    rhs=q_codes[:].bitcast(FP8X4),
-                    rhs_scale=q_scales[:],
-                    start=True,
-                    stop=True,
-                )
-                below = sb.tile([P, Q], F32, name="below%d" % chunk)
-                nc.scalar.activation(below[:], prod[:, 0:Q], ACT.Identity, bias=low_col[:, chunk : chunk + 1], scale=-1.0)
-                outside = sb.tile([P, Q], F32, name="outside%d" % chunk)
-                high_col = chunk * P + ROW
-                nc.vector.scalar_tensor_tensor(
-                    out=outside[:], in0=prod[:, 0:Q], scalar=high_t[:, high_col : high_col + 1], in1=below[:], op0=ALU.subtract, op1=ALU.max
-                )
-                nc.tensor.transpose(neg_margin[:, chunk * P : (chunk + 1) * P], outside[:], ident[:])
+        for chunk in range(CHUNKS):
+            prod = bank(2 + chunk, "prod%d" % chunk)
+            nc.tensor.matmul_mx(
+                out=prod[:, 0:Q],
+                lhsT=words[:, cols(chunk)].bitcast(FP4X4),
+                lhsT_scale=scales[chunk // 2][:, cols(chunk % 2)],
+                rhs=q_codes[:].bitcast(FP8X4),
+                rhs_scale=q_scales[:],
+                start=True,
+                stop=True,
+            )
+            below = sb.tile([P, Q], F32, name="below%d" % chunk)
+            nc.scalar.activation(below[:], prod[:, 0:Q], ACT.Identity, bias=low_col[:, chunk : chunk + 1], scale=-1.0)
+            outside = sb.tile([P, Q], F32, name="outside%d" % chunk)
+            high_col = chunk * P + ROW
+            nc.vector.scalar_tensor_tensor(
+                out=outside[:], in0=prod[:, 0:Q], scalar=high_t[:, high_col : high_col + 1], in1=below[:], op0=ALU.subtract, op1=ALU.max
+            )
+            nc.tensor.transpose(neg_margin[:, cols(chunk)], outside[:], ident[:])
+
+        neg_s = sb.tile([P, I], F32, name="neg_s")
         neg_max = sb.tile([P, 1], F32, name="neg_max")
         nc.vector.tensor_scalar(
             out=neg_s[:], in0=neg_margin[:], scalar1=lam_sb[:], scalar2=None, op0=ALU.mult, op1=ALU.min, accum_out=neg_max[:]
         )
-
         p_sb = sb.tile([P, I], F32, name="p_sb")
         row_sum = sb.tile([P, 1], F32, name="row_sum")
         nc.scalar.activation(p_sb[:], neg_s[:], ACT.Exp, bias=neg_max[:], scale=-1.0, accum_out=row_sum[:])
         inv_sum = sb.tile([P, 1], F32, name="inv_sum")
         nc.vector.reciprocal(inv_sum[:], row_sum[:])
-
         shares = []
         for h in range(2):
             share = sb.tile([P, HALF], F32, name="share%d" % h, align_bytes=64)
             nc.vector.tensor_scalar(
-                out=share[:], in0=p_sb[:, h * HALF : (h + 1) * HALF], scalar1=inv_sum[:], scalar2=128.0 * 128.0, op0=ALU.mult, op1=ALU.mult
+                out=share[:], in0=p_sb[:, h * HALF : (h + 1) * HALF], scalar1=inv_sum[:], scalar2=SHARE_SCALE, op0=ALU.mult, op1=ALU.mult
             )
             shares.append(share)
 
         def group_factors(share_t, h):
             group_sum = sb.tile([P, HALF // GROUP], F32, name="group_sum%d" % h)
             nc.vector.tensor_reduce(group_sum[:], share_t.rearrange("p (g j) -> p g j", j=GROUP), AX.X, ALU.add)
-            factor_t = sb.tile([P, HALF], F32, name="factor_t%d" % h, align_bytes=64)
+            spread = sb.tile([P, HALF], F32, name="spread%d" % h, align_bytes=64)
             nc.scalar.activation(
-                factor_t[:].rearrange("p (g j) -> p g j", j=GROUP),
+                spread[:].rearrange("p (g j) -> p g j", j=GROUP),
                 group_sum[:].unsqueeze(2).to_broadcast([P, HALF // GROUP, GROUP]),
                 ACT.Abs_reciprocal_sqrt,
                 bias=guard[:],
             )
-            return factor_t
+            return spread
 
         share_ps = bank(0, "share_ps")
         for c in range(2):
-            nc.tensor.transpose(share_ps[:, c * P : (c + 1) * P], shares[1][:, c * P : (c + 1) * P], ident[:])
+            nc.tensor.transpose(share_ps[:, cols(c)], shares[1][:, cols(c)], ident[:])
         share_blocks = sb.tile([P, HALF], F32, name="share_blocks", align_bytes=64)
         nc.vector.transpose(share_blocks[:], shares[0][:])
         factor_blocks = group_factors(share_blocks[:], 0)
@@ -175,8 +180,9 @@ def tile_attend_interval_balanced_counts_kernel(tc, query, keys_words, keys_scal
         nc.vector.transpose(factors[0][:], factor_blocks[:])
         factor_ps = bank(2, "factor_ps")
         for c in range(2):
-            nc.tensor.transpose(factor_ps[:, c * P : (c + 1) * P], factor_t[:, c * P : (c + 1) * P], ident[:])
+            nc.tensor.transpose(factor_ps[:, cols(c)], factor_t[:, cols(c)], ident[:])
         nc.scalar.copy(factors[1][:], factor_ps[:, 0:HALF])
+
         for h in range(2):
             nc.vector.tensor_tensor(placed[:].indirect(half_of(offs2_sb, h)), shares[h][:], factors[h][:], ALU.mult)
 

@@ -54,9 +54,9 @@ def tile_attend_interval_balanced_counts_kernel(tc, query, keys_words, keys_scal
         offs2_sb = sb.tile([P, I // 16], U16, name="offs2_sb")
         scale_win = sb.tile([P, T], U8, name="scale_win", tag="scales_then_placed")
         word_win = keys_pool.tile([P, T], U16, name="word_win", offset=0)
-        low_win = sb.tile([P, T], F32, name="low_win", tag="low_then_lam")
+        low_win = sb.tile([P, T], F32, name="low_win")
         high_win = high_pool.tile([P, T], F32, name="high_win", offset=0)
-        q_raw = sb.tile([P, PACK, Q], F32, name="q_raw", tag="query_then_old")
+        q_raw = sb.tile([P, PACK, Q], F32, name="q_raw")
         ident = sb.tile([P, P], F32, name="ident")
 
         nc.vector.memset(scale_win[:].bitcast(I32), 0)
@@ -86,13 +86,13 @@ def tile_attend_interval_balanced_counts_kernel(tc, query, keys_words, keys_scal
         nc.scalar.activation(high[:], high_win[:].indirect(offs_sb[:]), ACT.Copy)
         nc.vector.tensor_copy(lows[0][:], low_win[:].indirect(half_of(offs_sb, 0)))
         nc.scalar.activation(lows[1][:], low_win[:].indirect(half_of(offs_sb, 1)), ACT.Copy)
-        lam_sb = sb.tile([P, 1], F32, name="lam_sb", tag="low_then_lam")
+        lam_sb = high_pool.tile([P, 1], F32, name="lam_sb", offset=2 * PACK * Q)
         nc.sync.dma_start(out=lam_sb[:], in_=lam)
 
         q_bf = high_pool.tile([P, Q, PACK], BF16, name="q_bf", align_bytes=64, offset=0)
         nc.scalar.copy(q_bf[:], q_raw[:].rearrange("p j q -> p q j"))
 
-        words = sb.tile([P, I], U16, name="key_words", align_bytes=64)
+        words = sb.tile([P, I], U16, name="key_words", tag="words_then_old", align_bytes=64)
         nc.vector.tensor_copy(words[:], word_win[:].indirect(offs_sb[:]))
         scales = [high_pool.tile([P, HALF], U8, name="key_scales%d" % h, align_bytes=64, offset=h * HALF) for h in range(2)]
         q_codes = keys_pool.tile([P, Q], U32, name="q_codes", align_bytes=64, offset=0)
@@ -101,8 +101,6 @@ def tile_attend_interval_balanced_counts_kernel(tc, query, keys_words, keys_scal
         for h in range(2):
             nc.vector.tensor_copy(scales[h][:], scale_win[:].indirect(half_of(offs_sb, h)))
 
-        old_sb = sb.tile([P, M], F32, name="old_sb", tag="query_then_old")
-        nc.sync.dma_start(out=old_sb[:], in_=old)
         fade_sb = keys_pool.tile([P, 1], F32, name="fade_sb", offset=4 * Q)
         nc.sync.dma_start(out=fade_sb[:], in_=fade)
         placed = sb.tile([P, M], F32, name="placed", tag="scales_then_placed")
@@ -138,6 +136,9 @@ def tile_attend_interval_balanced_counts_kernel(tc, query, keys_words, keys_scal
             )
             nc.tensor.transpose(neg_margin[:, cols(chunk)], outside[:], ident[:])
 
+        old_sb = sb.tile([P, M], F32, name="old_sb", tag="words_then_old", align_bytes=64)
+        nc.sync.dma_start(out=old_sb[:], in_=old)
+
         neg_s = sb.tile([P, I], F32, name="neg_s")
         neg_max = sb.tile([P, 1], F32, name="neg_max")
         nc.vector.tensor_scalar(
@@ -160,12 +161,13 @@ def tile_attend_interval_balanced_counts_kernel(tc, query, keys_words, keys_scal
             group_sum = sb.tile([P, HALF // GROUP], F32, name="group_sum%d" % h)
             nc.vector.tensor_reduce(group_sum[:], share_t.rearrange("p (g j) -> p g j", j=GROUP), AX.X, ALU.add)
             spread = sb.tile([P, HALF], F32, name="spread%d" % h, align_bytes=64)
-            nc.scalar.activation(
-                spread[:].rearrange("p (g j) -> p g j", j=GROUP),
-                group_sum[:].unsqueeze(2).to_broadcast([P, HALF // GROUP, GROUP]),
-                ACT.Abs_reciprocal_sqrt,
-                bias=guard[:],
-            )
+            for c in range(2):
+                nc.scalar.activation(
+                    spread[:, cols(c)].rearrange("p (g j) -> p g j", j=GROUP),
+                    group_sum[:, c * K : (c + 1) * K].unsqueeze(2).to_broadcast([P, K, GROUP]),
+                    ACT.Abs_reciprocal_sqrt,
+                    bias=guard[:],
+                )
             return spread
 
         share_ps = bank(0, "share_ps")
@@ -177,7 +179,8 @@ def tile_attend_interval_balanced_counts_kernel(tc, query, keys_words, keys_scal
         factor_t = group_factors(share_ps[:, 0:HALF], 1)
 
         factors = [sb.tile([P, HALF], F32, name="factor%d" % h, align_bytes=64) for h in range(2)]
-        nc.vector.transpose(factors[0][:], factor_blocks[:])
+        for c in range(2):
+            nc.vector.transpose(factors[0][:, cols(c)], factor_blocks[:, cols(c)])
         factor_ps = bank(2, "factor_ps")
         for c in range(2):
             nc.tensor.transpose(factor_ps[:, cols(c)], factor_t[:, cols(c)], ident[:])

from contextlib import ExitStack

import concourse.mybir as mybir
from concourse.masks import make_identity

D, T, I, Q, K, M = 512, 2048, 512, 128, 16, 2048

F32 = mybir.dt.float32
BF16 = mybir.dt.bfloat16
I32 = mybir.dt.int32
U32 = mybir.dt.uint32
U16 = mybir.dt.uint16
U8 = mybir.dt.uint8
FP8X4 = mybir.dt.float8_e4m3fn_x4
FP4X4 = mybir.dt.float4_e2m1fn_x4
ALU = mybir.AluOpType
ACT = mybir.ActivationFunctionType
AX = mybir.AxisListType

P = 128
PACK = 4
CHUNKS = I // P
HALF = I // 2
GROUP = Q // K
ROW = P - 1
BANK = 512
SCALE_ROWS = 4
OUT_COLS = [384, 512, 512, 512, 128]
SHARE_SCALE = 128.0 * 128.0
TINY = 1e-30

FLOPS = 2 * D * Q * I
BYTES = 4 * D * Q + 2 * P * T + (D // 32) * T + 2 * 4 * T + 2 * 4 * Q + 2 * 4 * Q * M + 2 * 2 * P * (I // 16)


def tile_attend_interval_balanced_counts_kernel(tc, query, keys_words, keys_scales, lowend, highend, lam, old, fade, offs, offs2, out):
    nc = tc.nc
    with ExitStack() as ctx:
        sb = ctx.enter_context(tc.tile_pool(name="sb", bufs=1))
        keys_pool = ctx.enter_context(tc.tile_pool(name="keys_pool", bufs=1))
        high_pool = ctx.enter_context(tc.tile_pool(name="high_pool", bufs=1))
        ps = ctx.enter_context(tc.psum_pool(name="ps", bufs=1))

        def bank(n, name):
            return ps.tile([P, BANK], F32, name=name, tag="bank%d" % n)

        def half_of(list_tile, h):
            return list_tile[:, h * (HALF // 16) : (h + 1) * (HALF // 16)]

        def cols(chunk):
            return slice(chunk * P, (chunk + 1) * P)

        offs_sb = sb.tile([P, I // 16], U16, name="offs_sb")
        offs2_sb = sb.tile([P, I // 16], U16, name="offs2_sb")
        scale_win = sb.tile([P, T], U8, name="scale_win", tag="scales_then_placed")
        word_win = keys_pool.tile([P, T], U16, name="word_win", offset=0)
        low_win = sb.tile([P, T], F32, name="low_win")
        high_win = high_pool.tile([P, T], F32, name="high_win", offset=0)
        q_raw = sb.tile([P, PACK, Q], F32, name="q_raw")
        ident = sb.tile([P, P], F32, name="ident")

        nc.vector.memset(scale_win[:].bitcast(I32), 0)
        nc.vector.memset(high_win[0:ROW, :], 0.0)
        nc.vector.memset(low_win[0:ROW, :], 0.0)
        one = sb.tile([P, 1], F32, name="one")
        nc.gpsimd.memset(one[:], 1.0)
        make_identity(nc, ident[:])

        nc.sync.dma_start(offs_sb[:], offs)
        nc.sync.dma_start(out=high_win[ROW:P, :], in_=highend[0:1, :])
        nc.sync.dma_start(out=low_win[ROW:P, :], in_=lowend[0:1, :])
        nc.sync.dma_start(out=word_win[:].bitcast(I32), in_=keys_words[0].bitcast(I32))
        nc.sync.dma_start(out=q_raw[:], in_=query.rearrange("(p j) q -> p j q", j=PACK))
        for quad in range(P // 32):
            nc.sync.dma_start(
                out=scale_win[32 * quad : 32 * quad + SCALE_ROWS, :].bitcast(I32),
                in_=keys_scales[0, SCALE_ROWS * quad : SCALE_ROWS * (quad + 1), :].bitcast(I32),
            )
        nc.sync.dma_start(offs2_sb[:], offs2)

        guard = sb.tile([P, 1], F32, name="guard")
        nc.scalar.activation(guard[:], one[:], ACT.Copy, scale=TINY)

        lows = [sb.tile([P, HALF], F32, name="low%d" % h) for h in range(2)]
        high = sb.tile([P, I], F32, name="high")
        nc.scalar.activation(high[:], high_win[:].indirect(offs_sb[:]), ACT.Copy)
        nc.vector.tensor_copy(lows[0][:], low_win[:].indirect(half_of(offs_sb, 0)))
        nc.scalar.activation(lows[1][:], low_win[:].indirect(half_of(offs_sb, 1)), ACT.Copy)
        lam_sb = high_pool.tile([P, 1], F32, name="lam_sb", offset=2 * PACK * Q)
        nc.sync.dma_start(out=lam_sb[:], in_=lam)

        q_bf = high_pool.tile([P, Q, PACK], BF16, name="q_bf", align_bytes=64, offset=0)
        nc.scalar.copy(q_bf[:], q_raw[:].rearrange("p j q -> p q j"))

        words = sb.tile([P, I], U16, name="key_words", tag="words_then_old", align_bytes=64)
        nc.vector.tensor_copy(words[:], word_win[:].indirect(offs_sb[:]))
        scales = [high_pool.tile([P, HALF], U8, name="key_scales%d" % h, align_bytes=64, offset=h * HALF) for h in range(2)]
        q_codes = keys_pool.tile([P, Q], U32, name="q_codes", align_bytes=64, offset=0)
        q_scales = sb.tile([P, Q], U8, name="q_scales", align_bytes=64)
        nc.vector.quantize_mx(out=q_codes[:].bitcast(FP8X4), scales=q_scales[:], in_=q_bf[:].rearrange("p q j -> p (q j)"))
        for h in range(2):
            nc.vector.tensor_copy(scales[h][:], scale_win[:].indirect(half_of(offs_sb, h)))

        fade_sb = keys_pool.tile([P, 1], F32, name="fade_sb", offset=4 * Q)
        nc.sync.dma_start(out=fade_sb[:], in_=fade)
        placed = sb.tile([P, M], F32, name="placed", tag="scales_then_placed")
        nc.gpsimd.memset(placed[:], 0.0)

        low_t = bank(0, "low_t")
        high_t = bank(1, "high_t")
        for chunk in range(CHUNKS):
            nc.tensor.transpose(high_t[:, cols(chunk)], high[:, cols(chunk)], ident[:])
        for chunk in range(CHUNKS):
            nc.tensor.transpose(low_t[:, cols(chunk)], lows[chunk // 2][:, cols(chunk % 2)], ident[:])
        low_col = sb.tile([P, CHUNKS], F32, name="low_col")
        nc.scalar.copy(low_col[:], low_t[:, ROW::P])

        neg_margin = bank(6, "neg_margin")
        for chunk in range(CHUNKS):
            prod = bank(2 + chunk, "prod%d" % chunk)
            nc.tensor.matmul_mx(
                out=prod[:, 0:Q],
                lhsT=words[:, cols(chunk)].bitcast(FP4X4),
                lhsT_scale=scales[chunk // 2][:, cols(chunk % 2)],
                rhs=q_codes[:].bitcast(FP8X4),
                rhs_scale=q_scales[:],
                start=True,
                stop=True,
            )
            below = sb.tile([P, Q], F32, name="below%d" % chunk)
            nc.scalar.activation(below[:], prod[:, 0:Q], ACT.Identity, bias=low_col[:, chunk : chunk + 1], scale=-1.0)
            outside = sb.tile([P, Q], F32, name="outside%d" % chunk)
            high_col = chunk * P + ROW
            nc.vector.scalar_tensor_tensor(
                out=outside[:], in0=prod[:, 0:Q], scalar=high_t[:, high_col : high_col + 1], in1=below[:], op0=ALU.subtract, op1=ALU.max
            )
            nc.tensor.transpose(neg_margin[:, cols(chunk)], outside[:], ident[:])

        old_sb = sb.tile([P, M], F32, name="old_sb", tag="words_then_old", align_bytes=64)
        nc.sync.dma_start(out=old_sb[:], in_=old)

        neg_s = sb.tile([P, I], F32, name="neg_s")
        neg_max = sb.tile([P, 1], F32, name="neg_max")
        nc.vector.tensor_scalar(
            out=neg_s[:], in0=neg_margin[:], scalar1=lam_sb[:], scalar2=None, op0=ALU.mult, op1=ALU.min, accum_out=neg_max[:]
        )
        p_sb = sb.tile([P, I], F32, name="p_sb")
        row_sum = sb.tile([P, 1], F32, name="row_sum")
        nc.scalar.activation(p_sb[:], neg_s[:], ACT.Exp, bias=neg_max[:], scale=-1.0, accum_out=row_sum[:])
        inv_sum = sb.tile([P, 1], F32, name="inv_sum")
        nc.vector.reciprocal(inv_sum[:], row_sum[:])
        shares = []
        for h in range(2):
            share = sb.tile([P, HALF], F32, name="share%d" % h, align_bytes=64)
            nc.vector.tensor_scalar(
                out=share[:], in0=p_sb[:, h * HALF : (h + 1) * HALF], scalar1=inv_sum[:], scalar2=SHARE_SCALE, op0=ALU.mult, op1=ALU.mult
            )
            shares.append(share)

        def group_factors(share_t, h):
            group_sum = sb.tile([P, HALF // GROUP], F32, name="group_sum%d" % h)
            nc.vector.tensor_reduce(group_sum[:], share_t.rearrange("p (g j) -> p g j", j=GROUP), AX.X, ALU.add)
            spread = sb.tile([P, HALF], F32, name="spread%d" % h, align_bytes=64)
            for c in range(2):
                nc.scalar.activation(
                    spread[:, cols(c)].rearrange("p (g j) -> p g j", j=GROUP),
                    group_sum[:, c * K : (c + 1) * K].unsqueeze(2).to_broadcast([P, K, GROUP]),
                    ACT.Abs_reciprocal_sqrt,
                    bias=guard[:],
                )
            return spread

        share_ps = bank(0, "share_ps")
        for c in range(2):
            nc.tensor.transpose(share_ps[:, cols(c)], shares[1][:, cols(c)], ident[:])
        share_blocks = sb.tile([P, HALF], F32, name="share_blocks", align_bytes=64)
        nc.vector.transpose(share_blocks[:], shares[0][:])
        factor_blocks = group_factors(share_blocks[:], 0)
        factor_t = group_factors(share_ps[:, 0:HALF], 1)

        factors = [sb.tile([P, HALF], F32, name="factor%d" % h, align_bytes=64) for h in range(2)]
        for c in range(2):
            nc.vector.transpose(factors[0][:, cols(c)], factor_blocks[:, cols(c)])
        factor_ps = bank(2, "factor_ps")
        for c in range(2):
            nc.tensor.transpose(factor_ps[:, cols(c)], factor_t[:, cols(c)], ident[:])
        nc.scalar.copy(factors[1][:], factor_ps[:, 0:HALF])

        for h in range(2):
            nc.vector.tensor_tensor(placed[:].indirect(half_of(offs2_sb, h)), shares[h][:], factors[h][:], ALU.mult)

        col = 0
        for n, width in enumerate(OUT_COLS):
            result = sb.tile([P, width], F32, name="result%d" % n)
            nc.vector.scalar_tensor_tensor(
                out=result[:], in0=old_sb[:, col : col + width], scalar=fade_sb[:], in1=placed[:, col : col + width], op0=ALU.mult, op1=ALU.add
            )
            nc.sync.dma_start(out=out[:, col : col + width], in_=result[:])
            col += width
